import numpy as np
import ml_dtypes


def mxq(x, axis, fmt="e4m3"):
    dtype, down = {"e4m3": (ml_dtypes.float8_e4m3fn, 7), "e5m2": (ml_dtypes.float8_e5m2, 14)}[fmt]
    v = np.moveaxis(np.asarray(x, np.float32).astype(ml_dtypes.bfloat16).astype(np.float64), axis, -1)
    blocks = v.reshape(v.shape[:-1] + (-1, 32))
    amax = np.abs(blocks).max(-1, keepdims=True)
    byte = np.maximum(np.where(amax > 0, np.frexp(amax)[1] - 1 + 127, 0) - down, 1)
    scale = np.exp2(byte - 127.0)
    codes = (blocks / scale).astype(np.float32).astype(dtype).astype(np.float64)
    return np.moveaxis((codes * scale).reshape(v.shape), -1, axis)


WIDE = False


def mx_kscale(k):
    if not WIDE:
        return np.ones(k)
    levels = np.array([10, -10, 5, -5, 0])
    if k % 512:
        return np.exp2(np.random.permutation(np.resize(levels, k // 32))).repeat(32)
    a = np.empty((k // 512, 16))
    for p in range(k // 512):
        a[p, :8] = np.random.permutation(np.resize(levels, 8))
        for g in range(8):
            far = levels[np.abs(levels - a[p, g]) >= 10]
            a[p, g + 8] = far[np.random.randint(len(far))]
    return np.exp2(a.ravel()).repeat(32)


def f64(x):
    return np.asarray(x).astype(np.float64)


def striped(idx):
    return np.tile(idx.reshape(-1, 16).T, (8, 1)).astype(np.uint16)


def unstriped(offs):
    return offs[:16].T.reshape(-1).astype(np.int64)


def pack_weight(w):
    k, n = w.shape
    w = f64(np.asarray(w, np.float32).astype(ml_dtypes.bfloat16)).reshape(k // 32, 32, n)
    amax = np.abs(w).max(1)
    byte = np.clip(np.where(amax > 0, np.frexp(amax)[1] - 1 + 127 - 7, 1), 1, 254)
    scaled = (w * np.exp2(127.0 - byte)[:, None, :]).reshape(k, n).astype(np.float32)
    words = np.ascontiguousarray(scaled.reshape(k // 512, 128, 4, n).transpose(0, 1, 3, 2)).astype(ml_dtypes.float8_e4m3fn).view(np.uint8)
    return words, np.ascontiguousarray(byte.astype(np.uint8).reshape(k // 512, 16, n))


def unpack_weight(words, scales):
    g, p, n, _ = words.shape
    vals = np.ascontiguousarray(words).view(ml_dtypes.float8_e4m3fn).astype(np.float64) * np.repeat(np.exp2(scales.astype(np.float64) - 127.0), 8, axis=1)[..., None]
    return vals.transpose(0, 1, 3, 2).reshape(g * 512, n)


K, T, S, D, N = 512, 2048, 1024, 4, 256
P = 2 ** 7


def setup_inputs():
    n = np.random.standard_normal
    s = mx_kscale(K)[:, None]
    packed_xT = pack_weight(n((K, T)) * s)
    return {
        "x_words": packed_xT[0],
        "x_scales": packed_xT[1],
        "w1": (n((K, N)) / np.sqrt(K) / s).astype(np.float32),
        "w2": (n((K, N)) / np.sqrt(K) / s).astype(np.float32),
        "cot": (np.tile(np.random.uniform(0.2, 1.0, S), (P, 1))).astype(np.float32),
        "rx": (np.tile(n(S), (P, 1))).astype(np.float32),
        "ry": (np.tile(n(S), (P, 1))).astype(np.float32),
        "offs": striped(np.random.permutation(T)[:S]),
    }


def reference(x_words, x_scales, w1, w2, cot, rx, ry, offs):
    xq = unpack_weight(x_words, x_scales)[:, unstriped(offs)]
    y = mxq(f64(w1), 0, "e4m3").T @ xq
    z = mxq(f64(w2), 0, "e4m3").T @ xq
    da = f64(cot)[:1] * (f64(rx)[:1] * y + f64(ry)[:1] * z)
    aa = da.reshape(len(da), -1, D).sum(axis=2)
    ds = f64(cot)[:1] * (f64(rx)[:1] * z - (f64(ry)[:1] * y))
    ss = ds.reshape(len(ds), -1, D).sum(axis=2)
    nn = np.sqrt((aa) ** 2 + (ss) ** 2 + 0.1)
    cs = aa / nn
    sn = ss / nn
    rt = np.repeat(cs, D, axis=1) * f64(rx)[:1] - (np.repeat(sn, D, axis=1) * f64(ry)[:1])
    we = f64(cot)[:1] * ((y - rt) ** 2)
    return we.reshape(len(we), -1, D).sum(axis=2)

@@ -1,0 +1,284 @@
+from contextlib import ExitStack
+
+import concourse.mybir as mybir
+from concourse.masks import make_identity
+
+K, T, S, D, N = 512, 2048, 1024, 4, 256
+FLOPS = 2 * 2 * K * N * S
+
+F32 = mybir.dt.float32
+BF16 = mybir.dt.bfloat16
+I32 = mybir.dt.int32
+U32 = mybir.dt.uint32
+U16 = mybir.dt.uint16
+U8 = mybir.dt.uint8
+FP8X4 = mybir.dt.float8_e4m3fn_x4
+ACT = mybir.ActivationFunctionType
+MULT = mybir.AluOpType.mult
+ADD = mybir.AluOpType.add
+SUB = mybir.AluOpType.subtract
+
+P = 128
+PACK = 4
+BLOCKS = S // (D * P)
+HALVES = N // P
+EPS = 0.1
+NUDGE = 2.0 ** -58
+
+
+def tile_picked_yarap_en_p_kernel(tc, x_words, x_scales, w1, w2, cot, rx, ry, offs, out):
+    nc = tc.nc
+    with ExitStack() as ctx:
+        keep = ctx.enter_context(tc.tile_pool(name="keep", bufs=1))
+        psum = ctx.enter_context(tc.psum_pool(name="psum", bufs=1))
+
+        offsets = keep.tile([P, S // 16], U16, name="offsets")
+        nc.sync.dma_start(offsets[:], offs)
+        byte_table = keep.tile([P, T], U8, name="byte_table", align_bytes=64)
+        nc.gpsimd.memset(byte_table[:].bitcast(I32), 0)
+        rest = keep.tile([P, 2, BLOCKS, D], F32, name="rest")
+        weight = keep.tile([P, BLOCKS, D], F32, name="weight")
+        for c, row in enumerate((rx, ry)):
+            nc.gpsimd.dma_start(rest[:, c], row[0].rearrange("(b p d) -> p b d", b=BLOCKS, d=D))
+        nc.gpsimd.dma_start(weight[:], cot[0].rearrange("(b p d) -> p b d", b=BLOCKS, d=D))
+
+        for q in range(4):
+            nc.scalar.dma_start(byte_table[32 * q : 32 * q + 4, :].bitcast(I32), x_scales[0, 4 * q : 4 * q + 4, :].bitcast(I32))
+
+        w_raw = [keep.tile([P, PACK, N], F32, name=f"w_raw{i}") for i in range(2)]
+        for i, w in enumerate((w1, w2)):
+            nc.sync.dma_start(w_raw[i][:], w.rearrange("(p j) n -> p j n", j=PACK))
+        word_table = keep.tile([P, T], I32, name="word_table", align_bytes=64)
+        nc.sync.dma_start(word_table[:], x_words[0].rearrange("p n t -> p (n t)").bitcast(I32))
+
+        warm = keep.tile([P, 8], F32, name="warm")
+        warm_out = keep.tile([P, 8], F32, name="warm_out")
+        nc.vector.memset(warm[:], 1.0)
+        nc.scalar.activation(warm_out[:], warm[:], ACT.Abs_reciprocal_sqrt)
+
+        ident = keep.tile([P, P], F32, name="ident")
+        make_identity(nc, ident[:])
+
+        w_bf = [keep.tile([P, N, PACK], BF16, name=f"w_bf{i}", align_bytes=64) for i in range(2)]
+        w_codes = keep.tile([P, 2 * N], U32, name="w_codes", align_bytes=64)
+        w_bytes = keep.tile([P, 2 * N], U8, name="w_bytes", align_bytes=64)
+
+        def interleave(i):
+            nc.scalar.copy(w_bf[i][:], w_raw[i][:].rearrange("p j n -> p n j"))
+
+        def quantize(i):
+            cols = slice(i * N, (i + 1) * N)
+            nc.vector.quantize_mx(out=w_codes[:, cols].bitcast(FP8X4), scales=w_bytes[:, cols], in_=w_bf[i][:].rearrange("p n j -> p (n j)"))
+
+        interleave(0)
+
+        side = keep.tile([P, BLOCKS], F32, name="side")
+        pivot = keep.tile([P, BLOCKS], F32, name="pivot")
+        ry0_sq = keep.tile([P, BLOCKS], F32, name="ry0_sq")
+        inv_len = keep.tile([P, BLOCKS], F32, name="inv_len")
+        by_x = keep.tile([P, 2, BLOCKS, D], F32, name="by_x")
+        by_y = keep.tile([P, 2, BLOCKS, D], F32, name="by_y")
+        weight_n = keep.tile([P, BLOCKS, D], F32, name="weight_n")
+        nc.scalar.activation(side[:], rest[:, 0, :, 0], ACT.Sign, bias=NUDGE / 4)
+        nc.scalar.activation(ry0_sq[:], rest[:, 1, :, 0], ACT.Square)
+        for b in range(BLOCKS):
+            nc.scalar.activation(pivot[:, b : b + 1], side[:, b : b + 1], ACT.Identity, scale=NUDGE, bias=rest[:, 0, b, 0:1])
+        for b in range(BLOCKS):
+            nc.scalar.activation(by_y[:, :, b, :], rest[:, :, b, :], ACT.Copy, scale=rest[:, 1, b, 0:1])
+        for b in range(BLOCKS):
+            nc.scalar.activation(inv_len[:, b : b + 1], pivot[:, b : b + 1], ACT.Abs_reciprocal_sqrt, scale=pivot[:, b : b + 1], bias=ry0_sq[:, b : b + 1])
+        for b in range(BLOCKS):
+            nc.scalar.activation(by_x[:, :, b, :], rest[:, :, b, :], ACT.Copy, scale=pivot[:, b : b + 1])
+        for b in range(BLOCKS):
+            nc.scalar.activation(weight_n[:, b, :], weight[:, b, :], ACT.Copy, scale=inv_len[:, b : b + 1])
+
+        interleave(1)
+
+        picked_bytes = keep.tile([P, S], U8, name="picked_bytes", align_bytes=64)
+        dealt_bytes = keep.tile([P, BLOCKS, D, P], U8, name="dealt_bytes", align_bytes=64)
+        nc.vector.tensor_copy(picked_bytes[:], byte_table[:].indirect(offsets[:]))
+        quantize(0)
+        nc.vector.tensor_copy(dealt_bytes[:], picked_bytes[:].rearrange("p (b i d) -> p b d i", b=BLOCKS, d=D))
+        quantize(1)
+
+        turned = keep.tile([P, 2, BLOCKS, D], F32, name="turned")
+        coef = keep.tile([P, 2, BLOCKS, D], F32, name="coef")
+        nc.vector.tensor_tensor(turned[:, 0], by_x[:, 0], by_y[:, 1], ADD)
+        nc.vector.tensor_tensor(turned[:, 1], by_x[:, 1], by_y[:, 0], SUB)
+
+        picked_words = [keep.tile([P, D, P], U32, name=f"picked_words{b}", align_bytes=64) for b in range(BLOCKS)]
+        cols_per_block = S // 16 // BLOCKS
+
+        def gather_words(b):
+            part = offsets[:, b * cols_per_block : (b + 1) * cols_per_block]
+            nc.vector.tensor_copy(picked_words[b][:].rearrange("p d i -> p i d"), word_table[:].bitcast(U32).indirect(part))
+
+        gather_words(0)
+        nc.vector.tensor_tensor(
+            coef[:].rearrange("p c b d -> p c (b d)"),
+            turned[:].rearrange("p c b d -> p c (b d)"),
+            weight_n[:].rearrange("p b d -> p (b d)").unsqueeze(1).to_broadcast([P, 2, BLOCKS * D]),
+            MULT,
+        )
+        gather_words(1)
+
+        yz = [[psum.tile([P, 2, N], F32, name=f"yz{b}{d}", tag=f"bank{b * D + d}") for d in range(D)] for b in range(BLOCKS)]
+        for b in range(BLOCKS):
+            for d in range(D):
+                nc.tensor.matmul_mx(
+                    out=yz[b][d][:].rearrange("p c n -> p (c n)"),
+                    lhsT=picked_words[b][:, d, :].bitcast(FP8X4),
+                    lhsT_scale=dealt_bytes[:, b, d, :],
+                    rhs=w_codes[:].bitcast(FP8X4),
+                    rhs_scale=w_bytes[:],
+                    start=True,
+                    stop=True,
+                )
+
+        prods = keep.tile([P, 3, BLOCKS, D], F32, name="prods")
+        pairs = keep.tile([P, 3, BLOCKS, 2], F32, name="pairs")
+        sums = keep.tile([P, 3, BLOCKS], F32, name="sums")
+        form = keep.tile([P, 3, BLOCKS], F32, name="form")
+        diff = keep.tile([P, BLOCKS], F32, name="diff")
+        half_diff = keep.tile([P, BLOCKS], F32, name="half_diff")
+        c_eps = keep.tile([P, BLOCKS], F32, name="c_eps")
+        nc.gpsimd.tensor_tensor(
+            prods[:, 0:2].rearrange("p c b d -> p c (b d)"),
+            turned[:].rearrange("p c b d -> p c (b d)"),
+            coef[:, 0:1].rearrange("p c b d -> p c (b d)").to_broadcast([P, 2, BLOCKS * D]),
+            MULT,
+        )
+        nc.gpsimd.tensor_tensor(prods[:, 2], turned[:, 1], coef[:, 1], MULT)
+        nc.gpsimd.tensor_tensor(pairs[:], prods[:, :, :, 0:2], prods[:, :, :, 2:4], ADD)
+        nc.gpsimd.tensor_tensor(sums[:], pairs[:, :, :, 0], pairs[:, :, :, 1], ADD)
+        nc.gpsimd.tensor_tensor(form[:], sums[:], inv_len[:].unsqueeze(1).to_broadcast([P, 3, BLOCKS]), MULT)
+        nc.gpsimd.tensor_tensor(diff[:], form[:, 0], form[:, 2], SUB)
+        nc.gpsimd.tensor_scalar(half_diff[:], diff[:], 0.5, 0.0, MULT, ADD)
+        nc.gpsimd.tensor_scalar(c_eps[:], form[:, 2], -EPS, 0.0, MULT, ADD)
+
+        pq = [keep.tile([P, 2, N], F32, name=f"pq{b}") for b in range(BLOCKS)]
+        rot = [keep.tile([P, 2, N], F32, name=f"rot{b}") for b in range(BLOCKS)]
+        y_sq = [keep.tile([P, D, N], F32, name=f"y_sq{b}") for b in range(BLOCKS)]
+        energy = [keep.tile([P, D, N], F32, name=f"energy{b}") for b in range(BLOCKS)]
+        rot_sq = [keep.tile([P, 2, N], F32, name=f"rot_sq{b}") for b in range(BLOCKS)]
+        norm_sq = [keep.tile([P, N], F32, name=f"norm_sq{b}") for b in range(BLOCKS)]
+        inv = [keep.tile([P, N], F32, name=f"inv{b}") for b in range(BLOCKS)]
+        inv_sq = [keep.tile([P, N], F32, name=f"inv_sq{b}") for b in range(BLOCKS)]
+        level = [keep.tile([P, N], F32, name=f"level{b}") for b in range(BLOCKS)]
+        unit = [keep.tile([P, 2, N], F32, name=f"unit{b}") for b in range(BLOCKS)]
+        cross = [keep.tile([P, 2, N], F32, name=f"cross{b}") for b in range(BLOCKS)]
+        result = [keep.tile([P, HALVES, P], F32, name=f"result{b}") for b in range(BLOCKS)]
+        acc = [None] * BLOCKS
+
+        def a_of(b, d):
+            return coef[:, 0, b, d : d + 1]
+
+        def b_of(b, d):
+            return coef[:, 1, b, d : d + 1]
+
+        def square_y(b, d):
+            nc.scalar.activation(y_sq[b][:, d], yz[b][d][:, 0], ACT.Square)
+
+        def weigh(b, d):
+            nc.scalar.activation(energy[b][:, d], y_sq[b][:, d], ACT.Copy, scale=weight[:, b, d : d + 1])
+
+        def mac(dst, src, factor, prev, op=ADD):
+            nc.vector.scalar_tensor_tensor(dst, src, factor, prev, MULT, op)
+
+        def add_terms(b, terms, first, last):
+            for t, term in enumerate(terms):
+                for h in range(HALVES):
+                    nc.tensor.matmul(
+                        acc[b][:, h, :],
+                        lhsT=term[:, h * P : (h + 1) * P],
+                        rhs=ident[:],
+                        is_transpose=True,
+                        start=first and t == 0 and h == 0,
+                        stop=last and t == len(terms) - 1 and h == HALVES - 1,
+                    )
+
+        def heads(b):
+            nc.scalar.activation(pq[b][:, 0], yz[b][0][:, 0], ACT.Copy, scale=a_of(b, 0))
+            nc.scalar.activation(pq[b][:, 1], yz[b][1][:, 0], ACT.Copy, scale=b_of(b, 1))
+
+        def y_step(b, d):
+            if d >= 2:
+                mac(pq[b][:, 1], yz[b][d][:, 0], b_of(b, d), pq[b][:, 1])
+            mac(pq[b][:, 0], yz[b][d][:, 0], a_of(b, d), pq[b][:, 0])
+
+        def z_step(b, d):
+            if d == 0:
+                mac(rot[b][:, 1], yz[b][0][:, 1], a_of(b, 0), pq[b][:, 1], SUB)
+            else:
+                mac(rot[b][:, 0], yz[b][d][:, 1], b_of(b, d), pq[b][:, 0] if d == 1 else rot[b][:, 0])
+                mac(rot[b][:, 1], yz[b][d][:, 1], a_of(b, d), rot[b][:, 1])
+
+        def square_rot(b):
+            nc.scalar.activation(rot_sq[b][:], rot[b][:], ACT.Square)
+
+        def norm(b):
+            nc.vector.tensor_tensor(norm_sq[b][:], rot_sq[b][:, 0], rot_sq[b][:, 1], ADD)
+            nc.scalar.activation(inv[b][:], norm_sq[b][:], ACT.Abs_reciprocal_sqrt, bias=EPS)
+            nc.scalar.activation(inv_sq[b][:], inv[b][:], ACT.Square)
+            nc.scalar.activation(level[b][:], inv_sq[b][:], ACT.Identity, scale=c_eps[:, b : b + 1], bias=form[:, 2, b : b + 1])
+
+        def normalise(b):
+            nc.vector.tensor_tensor(unit[b][:], rot[b][:], inv[b][:].unsqueeze(1).to_broadcast([P, 2, N]), MULT)
+
+        def fold_sn(b):
+            mac(pq[b][:, 0], unit[b][:, 1], form[:, 1, b : b + 1], pq[b][:, 0])
+
+        def fold_cs(b):
+            mac(pq[b][:, 0], unit[b][:, 0], half_diff[:, b : b + 1], pq[b][:, 0], SUB)
+
+        def cross_term(b, c):
+            nc.vector.scalar_tensor_tensor(cross[b][:, c], pq[b][:, c], 2.0, unit[b][:, c], MULT, MULT)
+
+        def finish(b):
+            add_terms(b, [level[b], cross[b][:, 1], cross[b][:, 0]], False, True)
+            nc.scalar.copy(result[b][:], acc[b][:])
+            nc.sync.dma_start(out.rearrange("(h p) v -> p h v", p=P)[:, :, b * P : (b + 1) * P], result[b][:])
+
+        def open_acc(b):
+            acc[b] = psum.tile([P, HALVES, P], F32, name=f"acc{b}", tag=f"bank{b}")
+            add_terms(b, [energy[b][:, d] for d in range(D)], True, False)
+
+        heads(0)
+        square_y(0, 0)
+        for d in range(1, D):
+            y_step(0, d)
+            square_y(0, d)
+        heads(1)
+        for d in range(D):
+            square_y(1, d)
+        for d in range(D):
+            z_step(0, d)
+        square_rot(0)
+        for d in range(D):
+            weigh(0, d)
+        y_step(1, 1)
+        y_step(1, 2)
+        norm(0)
+        open_acc(0)
+        for d in range(D):
+            weigh(1, d)
+        y_step(1, 3)
+        z_step(1, 0)
+        z_step(1, 1)
+        normalise(0)
+        z_step(1, 2)
+        z_step(1, 3)
+        square_rot(1)
+        open_acc(1)
+        fold_sn(0)
+        cross_term(0, 1)
+        fold_cs(0)
+        norm(1)
+        cross_term(0, 0)
+        finish(0)
+        normalise(1)
+        fold_sn(1)
+        cross_term(1, 1)
+        fold_cs(1)
+        cross_term(1, 0)
+        finish(1)

@@ -17,6 +17,7 @@ ACT = mybir.ActivationFunctionType
 MULT = mybir.AluOpType.mult
 ADD = mybir.AluOpType.add
 SUB = mybir.AluOpType.subtract
+IS_GE = mybir.AluOpType.is_ge
 
 P = 128
 PACK = 4
@@ -33,27 +34,25 @@ def tile_picked_yarap_en_p_kernel(tc, x_words, x_scales, w1, w2, cot, rx, ry, of
         psum = ctx.enter_context(tc.psum_pool(name="psum", bufs=1))
 
         offsets = keep.tile([P, S // 16], U16, name="offsets")
-        nc.sync.dma_start(offsets[:], offs)
         byte_table = keep.tile([P, T], U8, name="byte_table", align_bytes=64)
-        nc.gpsimd.memset(byte_table[:].bitcast(I32), 0)
+        word_table = keep.tile([P, T], I32, name="word_table", align_bytes=64)
         rest = keep.tile([P, 2, BLOCKS, D], F32, name="rest")
         weight = keep.tile([P, BLOCKS, D], F32, name="weight")
-        for c, row in enumerate((rx, ry)):
-            nc.gpsimd.dma_start(rest[:, c], row[0].rearrange("(b p d) -> p b d", b=BLOCKS, d=D))
-        nc.gpsimd.dma_start(weight[:], cot[0].rearrange("(b p d) -> p b d", b=BLOCKS, d=D))
-
+        w_raw = [keep.tile([P, PACK, N], F32, name=f"w_raw{i}") for i in range(2)]
+        nc.vector.memset(byte_table[:].bitcast(I32), 0)
+        warm = keep.tile([P, 8], F32, name="warm")
+        nc.vector.memset(warm[:], 1.0)
         for q in range(4):
             nc.scalar.dma_start(byte_table[32 * q : 32 * q + 4, :].bitcast(I32), x_scales[0, 4 * q : 4 * q + 4, :].bitcast(I32))
-
-        w_raw = [keep.tile([P, PACK, N], F32, name=f"w_raw{i}") for i in range(2)]
-        for i, w in enumerate((w1, w2)):
-            nc.sync.dma_start(w_raw[i][:], w.rearrange("(p j) n -> p j n", j=PACK))
-        word_table = keep.tile([P, T], I32, name="word_table", align_bytes=64)
+        nc.sync.dma_start(offsets[:], offs)
+        for c, row in enumerate((rx, ry)):
+            nc.sync.dma_start(rest[:, c], row[0].rearrange("(b p d) -> p b d", b=BLOCKS, d=D))
+        nc.sync.dma_start(weight[:], cot[0].rearrange("(b p d) -> p b d", b=BLOCKS, d=D))
+        nc.sync.dma_start(w_raw[0][:], w1.rearrange("(p j) n -> p j n", j=PACK))
         nc.sync.dma_start(word_table[:], x_words[0].rearrange("p n t -> p (n t)").bitcast(I32))
+        nc.sync.dma_start(w_raw[1][:], w2.rearrange("(p j) n -> p j n", j=PACK))
 
-        warm = keep.tile([P, 8], F32, name="warm")
         warm_out = keep.tile([P, 8], F32, name="warm_out")
-        nc.vector.memset(warm[:], 1.0)
         nc.scalar.activation(warm_out[:], warm[:], ACT.Abs_reciprocal_sqrt)
 
         ident = keep.tile([P, P], F32, name="ident")
@@ -70,42 +69,36 @@ def tile_picked_yarap_en_p_kernel(tc, x_words, x_scales, w1, w2, cot, rx, ry, of
             cols = slice(i * N, (i + 1) * N)
             nc.vector.quantize_mx(out=w_codes[:, cols].bitcast(FP8X4), scales=w_bytes[:, cols], in_=w_bf[i][:].rearrange("p n j -> p (n j)"))
 
-        interleave(0)
-
         side = keep.tile([P, BLOCKS], F32, name="side")
         pivot = keep.tile([P, BLOCKS], F32, name="pivot")
-        ry0_sq = keep.tile([P, BLOCKS], F32, name="ry0_sq")
         inv_len = keep.tile([P, BLOCKS], F32, name="inv_len")
         by_x = keep.tile([P, 2, BLOCKS, D], F32, name="by_x")
         by_y = keep.tile([P, 2, BLOCKS, D], F32, name="by_y")
         weight_n = keep.tile([P, BLOCKS, D], F32, name="weight_n")
-        nc.scalar.activation(side[:], rest[:, 0, :, 0], ACT.Sign, bias=NUDGE / 4)
-        nc.scalar.activation(ry0_sq[:], rest[:, 1, :, 0], ACT.Square)
+        turned = keep.tile([P, 2, BLOCKS, D], F32, name="turned")
+        coef = keep.tile([P, 2, BLOCKS, D], F32, name="coef")
+        whole = [P, 2, BLOCKS, D]
+        nc.vector.tensor_scalar(side[:], rest[:, 0, :, 0], 0.0, 2 * NUDGE, IS_GE, MULT)
+        nc.vector.tensor_tensor(by_y[:], rest[:], rest[:, 1:2, :, 0:1].to_broadcast(whole), MULT)
+        nc.vector.scalar_tensor_tensor(pivot[:], side[:], -NUDGE, rest[:, 0, :, 0], ADD, ADD)
+        nc.vector.tensor_tensor(by_x[:], rest[:], pivot[:].unsqueeze(1).unsqueeze(3).to_broadcast(whole), MULT)
+        nc.vector.tensor_tensor(turned[:, 0], by_x[:, 0], by_y[:, 1], ADD)
+        nc.vector.tensor_tensor(turned[:, 1], by_x[:, 1], by_y[:, 0], SUB)
         for b in range(BLOCKS):
-            nc.scalar.activation(pivot[:, b : b + 1], side[:, b : b + 1], ACT.Identity, scale=NUDGE, bias=rest[:, 0, b, 0:1])
-        for b in range(BLOCKS):
-            nc.scalar.activation(by_y[:, :, b, :], rest[:, :, b, :], ACT.Copy, scale=rest[:, 1, b, 0:1])
-        for b in range(BLOCKS):
-            nc.scalar.activation(inv_len[:, b : b + 1], pivot[:, b : b + 1], ACT.Abs_reciprocal_sqrt, scale=pivot[:, b : b + 1], bias=ry0_sq[:, b : b + 1])
-        for b in range(BLOCKS):
-            nc.scalar.activation(by_x[:, :, b, :], rest[:, :, b, :], ACT.Copy, scale=pivot[:, b : b + 1])
+            nc.scalar.activation(inv_len[:, b : b + 1], pivot[:, b : b + 1], ACT.Abs_reciprocal_sqrt, scale=pivot[:, b : b + 1], bias=by_y[:, 1, b, 0:1])
         for b in range(BLOCKS):
             nc.scalar.activation(weight_n[:, b, :], weight[:, b, :], ACT.Copy, scale=inv_len[:, b : b + 1])
-
-        interleave(1)
+        interleave(0)
 
         picked_bytes = keep.tile([P, S], U8, name="picked_bytes", align_bytes=64)
         dealt_bytes = keep.tile([P, BLOCKS, D, P], U8, name="dealt_bytes", align_bytes=64)
         nc.vector.tensor_copy(picked_bytes[:], byte_table[:].indirect(offsets[:]))
-        quantize(0)
-        nc.vector.tensor_copy(dealt_bytes[:], picked_bytes[:].rearrange("p (b i d) -> p b d i", b=BLOCKS, d=D))
-        quantize(1)
-
-        turned = keep.tile([P, 2, BLOCKS, D], F32, name="turned")
-        coef = keep.tile([P, 2, BLOCKS, D], F32, name="coef")
-        nc.vector.tensor_tensor(turned[:, 0], by_x[:, 0], by_y[:, 1], ADD)
-        nc.vector.tensor_tensor(turned[:, 1], by_x[:, 1], by_y[:, 0], SUB)
-
+        nc.vector.tensor_tensor(
+            coef[:].rearrange("p c b d -> p c (b d)"),
+            turned[:].rearrange("p c b d -> p c (b d)"),
+            weight_n[:].rearrange("p b d -> p (b d)").unsqueeze(1).to_broadcast([P, 2, BLOCKS * D]),
+            MULT,
+        )
         picked_words = [keep.tile([P, D, P], U32, name=f"picked_words{b}", align_bytes=64) for b in range(BLOCKS)]
         cols_per_block = S // 16 // BLOCKS
 
@@ -113,50 +106,49 @@ def tile_picked_yarap_en_p_kernel(tc, x_words, x_scales, w1, w2, cot, rx, ry, of
             part = offsets[:, b * cols_per_block : (b + 1) * cols_per_block]
             nc.vector.tensor_copy(picked_words[b][:].rearrange("p d i -> p i d"), word_table[:].bitcast(U32).indirect(part))
 
-        gather_words(0)
-        nc.vector.tensor_tensor(
-            coef[:].rearrange("p c b d -> p c (b d)"),
-            turned[:].rearrange("p c b d -> p c (b d)"),
-            weight_n[:].rearrange("p b d -> p (b d)").unsqueeze(1).to_broadcast([P, 2, BLOCKS * D]),
-            MULT,
-        )
-        gather_words(1)
-
-        yz = [[psum.tile([P, 2, N], F32, name=f"yz{b}{d}", tag=f"bank{b * D + d}") for d in range(D)] for b in range(BLOCKS)]
-        for b in range(BLOCKS):
-            for d in range(D):
-                nc.tensor.matmul_mx(
-                    out=yz[b][d][:].rearrange("p c n -> p (c n)"),
-                    lhsT=picked_words[b][:, d, :].bitcast(FP8X4),
-                    lhsT_scale=dealt_bytes[:, b, d, :],
-                    rhs=w_codes[:].bitcast(FP8X4),
-                    rhs_scale=w_bytes[:],
-                    start=True,
-                    stop=True,
-                )
+        def deal_bytes(b):
+            nc.vector.tensor_copy(dealt_bytes[:, b], picked_bytes[:, b * D * P : (b + 1) * D * P].rearrange("p (i d) -> p d i", d=D))
 
         prods = keep.tile([P, 3, BLOCKS, D], F32, name="prods")
-        pairs = keep.tile([P, 3, BLOCKS, 2], F32, name="pairs")
         sums = keep.tile([P, 3, BLOCKS], F32, name="sums")
         form = keep.tile([P, 3, BLOCKS], F32, name="form")
         diff = keep.tile([P, BLOCKS], F32, name="diff")
-        half_diff = keep.tile([P, BLOCKS], F32, name="half_diff")
+        minus_b = keep.tile([P, BLOCKS], F32, name="minus_b")
         c_eps = keep.tile([P, BLOCKS], F32, name="c_eps")
-        nc.gpsimd.tensor_tensor(
-            prods[:, 0:2].rearrange("p c b d -> p c (b d)"),
-            turned[:].rearrange("p c b d -> p c (b d)"),
-            coef[:, 0:1].rearrange("p c b d -> p c (b d)").to_broadcast([P, 2, BLOCKS * D]),
-            MULT,
-        )
-        nc.gpsimd.tensor_tensor(prods[:, 2], turned[:, 1], coef[:, 1], MULT)
-        nc.gpsimd.tensor_tensor(pairs[:], prods[:, :, :, 0:2], prods[:, :, :, 2:4], ADD)
-        nc.gpsimd.tensor_tensor(sums[:], pairs[:, :, :, 0], pairs[:, :, :, 1], ADD)
-        nc.gpsimd.tensor_tensor(form[:], sums[:], inv_len[:].unsqueeze(1).to_broadcast([P, 3, BLOCKS]), MULT)
-        nc.gpsimd.tensor_tensor(diff[:], form[:, 0], form[:, 2], SUB)
-        nc.gpsimd.tensor_scalar(half_diff[:], diff[:], 0.5, 0.0, MULT, ADD)
-        nc.gpsimd.tensor_scalar(c_eps[:], form[:, 2], -EPS, 0.0, MULT, ADD)
+        deal_bytes(0)
+        nc.vector.tensor_tensor(prods[:, 0:2], turned[:], coef[:], MULT)
+        nc.vector.tensor_tensor(prods[:, 2], turned[:, 1], coef[:, 0], MULT)
+        quantize(0)
+        nc.vector.tensor_reduce(sums[:], prods[:], mybir.AxisListType.X, ADD)
+        for b in range(BLOCKS):
+            nc.scalar.activation(form[:, :, b], sums[:, :, b], ACT.Copy, scale=inv_len[:, b : b + 1])
+        for b in range(BLOCKS):
+            nc.scalar.activation(diff[:, b : b + 1], form[:, 1, b : b + 1], ACT.Identity, scale=-1.0, bias=form[:, 0, b : b + 1])
+        nc.scalar.activation(minus_b[:], form[:, 2], ACT.Copy, scale=-1.0)
+        nc.scalar.activation(c_eps[:], form[:, 1], ACT.Copy, scale=-EPS)
+        interleave(1)
+        gather_words(0)
+        deal_bytes(1)
+        gather_words(1)
+        quantize(1)
 
-        pq = [keep.tile([P, 2, N], F32, name=f"pq{b}") for b in range(BLOCKS)]
+        banks = [[psum.tile([P, 2, N], F32, name=f"yz{b}{e}", tag=f"bank{D * b + e}") for e in range(D)] for b in range(BLOCKS)]
+
+        def yz(b, i, d):
+            return banks[0][2 * i + d // 2][:, d % 2] if b == 0 else banks[1][d][:, i]
+
+        def product(dst, b, d, cols):
+            nc.tensor.matmul_mx(
+                out=dst,
+                lhsT=picked_words[b][:, d, :].bitcast(FP8X4),
+                lhsT_scale=dealt_bytes[:, b, d, :],
+                rhs=w_codes[:, cols].bitcast(FP8X4),
+                rhs_scale=w_bytes[:, cols],
+                start=True,
+                stop=True,
+            )
+
+        sums_yz = [keep.tile([P, 2, 2, N], F32, name=f"sums_yz{b}") for b in range(BLOCKS)]
         rot = [keep.tile([P, 2, N], F32, name=f"rot{b}") for b in range(BLOCKS)]
         y_sq = [keep.tile([P, D, N], F32, name=f"y_sq{b}") for b in range(BLOCKS)]
         energy = [keep.tile([P, D, N], F32, name=f"energy{b}") for b in range(BLOCKS)]
@@ -165,25 +157,25 @@ def tile_picked_yarap_en_p_kernel(tc, x_words, x_scales, w1, w2, cot, rx, ry, of
         inv = [keep.tile([P, N], F32, name=f"inv{b}") for b in range(BLOCKS)]
         inv_sq = [keep.tile([P, N], F32, name=f"inv_sq{b}") for b in range(BLOCKS)]
         level = [keep.tile([P, N], F32, name=f"level{b}") for b in range(BLOCKS)]
+        quad = [keep.tile([P, N], F32, name=f"quad{b}") for b in range(BLOCKS)]
         unit = [keep.tile([P, 2, N], F32, name=f"unit{b}") for b in range(BLOCKS)]
         cross = [keep.tile([P, 2, N], F32, name=f"cross{b}") for b in range(BLOCKS)]
         result = [keep.tile([P, HALVES, P], F32, name=f"result{b}") for b in range(BLOCKS)]
         acc = [None] * BLOCKS
 
-        def a_of(b, d):
-            return coef[:, 0, b, d : d + 1]
-
-        def b_of(b, d):
-            return coef[:, 1, b, d : d + 1]
+        def square_pair(e):
+            nc.scalar.activation(y_sq[0][:, 2 * e : 2 * e + 2], banks[0][e][:], ACT.Square)
 
         def square_y(b, d):
-            nc.scalar.activation(y_sq[b][:, d], yz[b][d][:, 0], ACT.Square)
+            nc.scalar.activation(y_sq[b][:, d], yz(b, 0, d), ACT.Square)
 
         def weigh(b, d):
-            nc.scalar.activation(energy[b][:, d], y_sq[b][:, d], ACT.Copy, scale=weight[:, b, d : d + 1])
-
-        def mac(dst, src, factor, prev, op=ADD):
-            nc.vector.scalar_tensor_tensor(dst, src, factor, prev, MULT, op)
+            bias = form[:, 1, b : b + 1] if d == D - 1 else 0.0
+            if (b, d) in ((0, 0), (0, 1), (0, 2), (0, 3)):
+                nc.gpsimd.tensor_scalar(energy[b][:, d], y_sq[b][:, d], weight[:, b, d : d + 1], bias, MULT, ADD)
+            else:
+                func = ACT.Identity if d == D - 1 else ACT.Copy
+                nc.scalar.activation(energy[b][:, d], y_sq[b][:, d], func, scale=weight[:, b, d : d + 1], bias=bias)
 
         def add_terms(b, terms, first, last):
             for t, term in enumerate(terms):
@@ -197,45 +189,56 @@ def tile_picked_yarap_en_p_kernel(tc, x_words, x_scales, w1, w2, cot, rx, ry, of
                         stop=last and t == len(terms) - 1 and h == HALVES - 1,
                     )
 
-        def heads(b):
-            nc.scalar.activation(pq[b][:, 0], yz[b][0][:, 0], ACT.Copy, scale=a_of(b, 0))
-            nc.scalar.activation(pq[b][:, 1], yz[b][1][:, 0], ACT.Copy, scale=b_of(b, 1))
+        def head(b, c, i):
+            nc.scalar.activation(sums_yz[b][:, c, i], yz(b, i, c), ACT.Copy, scale=coef[:, c, b, c : c + 1])
 
-        def y_step(b, d):
-            if d >= 2:
-                mac(pq[b][:, 1], yz[b][d][:, 0], b_of(b, d), pq[b][:, 1])
-            mac(pq[b][:, 0], yz[b][d][:, 0], a_of(b, d), pq[b][:, 0])
+        def mac(dst, b, i, c, d, prev, op=ADD):
+            nc.vector.scalar_tensor_tensor(dst, yz(b, i, d), coef[:, c, b, d : d + 1], prev, MULT, op)
 
-        def z_step(b, d):
-            if d == 0:
-                mac(rot[b][:, 1], yz[b][0][:, 1], a_of(b, 0), pq[b][:, 1], SUB)
-            else:
-                mac(rot[b][:, 0], yz[b][d][:, 1], b_of(b, d), pq[b][:, 0] if d == 1 else rot[b][:, 0])
-                mac(rot[b][:, 1], yz[b][d][:, 1], a_of(b, d), rot[b][:, 1])
+        def sum_up(b, i):
+            for c, d in ((1, 2), (0, 2), (1, 3), (0, 3), (0, 1)):
+                mac(sums_yz[b][:, c, i], b, i, c, d, sums_yz[b][:, c, i])
+
+        by_b = keep.tile([P, D - 1, 2, N], F32, name="by_b")
+        part = keep.tile([P, 2, N], F32, name="part")
+
+        def scale_bank(dst, c, d):
+            nc.scalar.activation(dst, banks[1][d][:], ACT.Copy, scale=coef[:, c, 1, d : d + 1])
+
+        def mac_bank(c, d, prev):
+            nc.vector.scalar_tensor_tensor(sums_yz[1][:, c], banks[1][d][:], coef[:, c, 1, d : d + 1], prev, MULT, ADD)
+
+        def combine(engine, b):
+            engine.tensor_tensor(rot[b][:, 0], sums_yz[b][:, 0, 0], sums_yz[b][:, 1, 1], ADD)
+            engine.tensor_tensor(rot[b][:, 1], sums_yz[b][:, 0, 1], sums_yz[b][:, 1, 0], SUB)
 
         def square_rot(b):
             nc.scalar.activation(rot_sq[b][:], rot[b][:], ACT.Square)
 
-        def norm(b):
-            nc.vector.tensor_tensor(norm_sq[b][:], rot_sq[b][:, 0], rot_sq[b][:, 1], ADD)
+        def norm(engine, b):
+            engine.tensor_tensor(norm_sq[b][:], rot_sq[b][:, 0], rot_sq[b][:, 1], ADD)
+
+        def invert(b):
             nc.scalar.activation(inv[b][:], norm_sq[b][:], ACT.Abs_reciprocal_sqrt, bias=EPS)
             nc.scalar.activation(inv_sq[b][:], inv[b][:], ACT.Square)
-            nc.scalar.activation(level[b][:], inv_sq[b][:], ACT.Identity, scale=c_eps[:, b : b + 1], bias=form[:, 2, b : b + 1])
+
+        def make_level(b):
+            nc.scalar.activation(level[b][:], rot_sq[b][:, 0], ACT.Identity, scale=diff[:, b : b + 1], bias=c_eps[:, b : b + 1])
 
         def normalise(b):
             nc.vector.tensor_tensor(unit[b][:], rot[b][:], inv[b][:].unsqueeze(1).to_broadcast([P, 2, N]), MULT)
 
-        def fold_sn(b):
-            mac(pq[b][:, 0], unit[b][:, 1], form[:, 1, b : b + 1], pq[b][:, 0])
+        def fold(b):
+            nc.vector.scalar_tensor_tensor(sums_yz[b][:, 0, 0], unit[b][:, 1], minus_b[:, b : b + 1], sums_yz[b][:, 0, 0], MULT, SUB)
 
-        def fold_cs(b):
-            mac(pq[b][:, 0], unit[b][:, 0], half_diff[:, b : b + 1], pq[b][:, 0], SUB)
+        def quad_term(b):
+            nc.vector.tensor_tensor(quad[b][:], level[b][:], inv_sq[b][:], MULT)
 
-        def cross_term(b, c):
-            nc.vector.scalar_tensor_tensor(cross[b][:, c], pq[b][:, c], 2.0, unit[b][:, c], MULT, MULT)
+        def cross_terms(b, cs):
+            nc.vector.scalar_tensor_tensor(cross[b][:, cs], sums_yz[b][:, cs, 0], 2.0, unit[b][:, cs], MULT, MULT)
 
-        def finish(b):
-            add_terms(b, [level[b], cross[b][:, 1], cross[b][:, 0]], False, True)
+        def finish(b, terms):
+            add_terms(b, terms, False, True)
             nc.scalar.copy(result[b][:], acc[b][:])
             nc.sync.dma_start(out.rearrange("(h p) v -> p h v", p=P)[:, :, b * P : (b + 1) * P], result[b][:])
 
@@ -243,42 +246,58 @@ def tile_picked_yarap_en_p_kernel(tc, x_words, x_scales, w1, w2, cot, rx, ry, of
             acc[b] = psum.tile([P, HALVES, P], F32, name=f"acc{b}", tag=f"bank{b}")
             add_terms(b, [energy[b][:, d] for d in range(D)], True, False)
 
-        heads(0)
-        square_y(0, 0)
-        for d in range(1, D):
-            y_step(0, d)
-            square_y(0, d)
-        heads(1)
+        for i in range(2):
+            for d in range(D):
+                product(yz(0, i, d), 0, d, slice(i * N, (i + 1) * N))
         for d in range(D):
-            square_y(1, d)
-        for d in range(D):
-            z_step(0, d)
+            product(banks[1][d][:].rearrange("p i n -> p (i n)"), 1, d, slice(0, 2 * N))
+        head(0, 0, 0)
+        head(0, 1, 0)
+        square_pair(0)
+        head(0, 0, 1)
+        head(0, 1, 1)
+        sum_up(0, 0)
+        square_pair(1)
+        scale_bank(sums_yz[1][:, 0], 0, 0)
+        scale_bank(sums_yz[1][:, 1], 1, 1)
+        square_y(1, 1)
+        square_y(1, 0)
+        sum_up(0, 1)
+        combine(nc.gpsimd, 0)
         square_rot(0)
-        for d in range(D):
-            weigh(0, d)
-        y_step(1, 1)
-        y_step(1, 2)
-        norm(0)
-        open_acc(0)
-        for d in range(D):
-            weigh(1, d)
-        y_step(1, 3)
-        z_step(1, 0)
-        z_step(1, 1)
-        normalise(0)
-        z_step(1, 2)
-        z_step(1, 3)
+        mac_bank(0, 2, sums_yz[1][:, 0])
+        mac_bank(1, 2, sums_yz[1][:, 1])
+        mac_bank(0, 3, sums_yz[1][:, 0])
+        norm(nc.vector, 0)
+        invert(0)
+        make_level(0)
+        mac_bank(1, 3, sums_yz[1][:, 1])
+        mac_bank(0, 1, sums_yz[1][:, 0])
+        combine(nc.vector, 1)
         square_rot(1)
-        open_acc(1)
-        fold_sn(0)
-        cross_term(0, 1)
-        fold_cs(0)
-        norm(1)
-        cross_term(0, 0)
-        finish(0)
+        normalise(0)
+        quad_term(0)
+        fold(0)
+        norm(nc.vector, 1)
+        invert(1)
+        make_level(1)
+        cross_terms(0, slice(0, 2))
         normalise(1)
-        fold_sn(1)
-        cross_term(1, 1)
-        fold_cs(1)
-        cross_term(1, 0)
-        finish(1)
+        quad_term(1)
+        fold(1)
+        cross_terms(1, slice(1, 2))
+        cross_terms(1, slice(0, 1))
+        square_y(1, 2)
+        square_y(1, 3)
+        weigh(0, 0)
+        weigh(0, 1)
+        weigh(0, 2)
+        weigh(0, 3)
+        weigh(1, 0)
+        weigh(1, 1)
+        weigh(1, 2)
+        weigh(1, 3)
+        open_acc(0)
+        open_acc(1)
+        finish(0, [quad[0], cross[0][:, 0], cross[0][:, 1]])
+        finish(1, [quad[1], cross[1][:, 1], cross[1][:, 0]])

from contextlib import ExitStack

import concourse.mybir as mybir
from concourse.masks import make_identity

K, T, S, D, N = 512, 2048, 1024, 4, 256
FLOPS = 2 * 2 * K * N * S

F32 = mybir.dt.float32
BF16 = mybir.dt.bfloat16
I32 = mybir.dt.int32
U32 = mybir.dt.uint32
U16 = mybir.dt.uint16
U8 = mybir.dt.uint8
FP8X4 = mybir.dt.float8_e4m3fn_x4
ACT = mybir.ActivationFunctionType
MULT = mybir.AluOpType.mult
ADD = mybir.AluOpType.add
SUB = mybir.AluOpType.subtract
IS_GE = mybir.AluOpType.is_ge

P = 128
PACK = 4
BLOCKS = S // (D * P)
HALVES = N // P
EPS = 0.1
NUDGE = 2.0 ** -58


def tile_picked_yarap_en_p_kernel(tc, x_words, x_scales, w1, w2, cot, rx, ry, offs, out):
    nc = tc.nc
    with ExitStack() as ctx:
        keep = ctx.enter_context(tc.tile_pool(name="keep", bufs=1))
        psum = ctx.enter_context(tc.psum_pool(name="psum", bufs=1))

        offsets = keep.tile([P, S // 16], U16, name="offsets")
        byte_table = keep.tile([P, T], U8, name="byte_table", align_bytes=64)
        word_table = keep.tile([P, T], I32, name="word_table", align_bytes=64)
        rest = keep.tile([P, 2, BLOCKS, D], F32, name="rest")
        weight = keep.tile([P, BLOCKS, D], F32, name="weight")
        w_raw = [keep.tile([P, PACK, N], F32, name=f"w_raw{i}") for i in range(2)]
        nc.vector.memset(byte_table[:].bitcast(I32), 0)
        warm = keep.tile([P, 8], F32, name="warm")
        nc.vector.memset(warm[:], 1.0)
        for q in range(4):
            nc.scalar.dma_start(byte_table[32 * q : 32 * q + 4, :].bitcast(I32), x_scales[0, 4 * q : 4 * q + 4, :].bitcast(I32))
        nc.sync.dma_start(offsets[:], offs)
        for c, row in enumerate((rx, ry)):
            nc.sync.dma_start(rest[:, c], row[0].rearrange("(b p d) -> p b d", b=BLOCKS, d=D))
        nc.sync.dma_start(weight[:], cot[0].rearrange("(b p d) -> p b d", b=BLOCKS, d=D))
        nc.sync.dma_start(w_raw[0][:], w1.rearrange("(p j) n -> p j n", j=PACK))
        nc.sync.dma_start(word_table[:], x_words[0].rearrange("p n t -> p (n t)").bitcast(I32))
        nc.sync.dma_start(w_raw[1][:], w2.rearrange("(p j) n -> p j n", j=PACK))

        warm_out = keep.tile([P, 8], F32, name="warm_out")
        nc.scalar.activation(warm_out[:], warm[:], ACT.Abs_reciprocal_sqrt)

        ident = keep.tile([P, P], F32, name="ident")
        make_identity(nc, ident[:])

        w_bf = [keep.tile([P, N, PACK], BF16, name=f"w_bf{i}", align_bytes=64) for i in range(2)]
        w_codes = keep.tile([P, 2 * N], U32, name="w_codes", align_bytes=64)
        w_bytes = keep.tile([P, 2 * N], U8, name="w_bytes", align_bytes=64)

        def interleave(i):
            nc.scalar.copy(w_bf[i][:], w_raw[i][:].rearrange("p j n -> p n j"))

        def quantize(i):
            cols = slice(i * N, (i + 1) * N)
            nc.vector.quantize_mx(out=w_codes[:, cols].bitcast(FP8X4), scales=w_bytes[:, cols], in_=w_bf[i][:].rearrange("p n j -> p (n j)"))

        side = keep.tile([P, BLOCKS], F32, name="side")
        pivot = keep.tile([P, BLOCKS], F32, name="pivot")
        inv_len = keep.tile([P, BLOCKS], F32, name="inv_len")
        by_x = keep.tile([P, 2, BLOCKS, D], F32, name="by_x")
        by_y = keep.tile([P, 2, BLOCKS, D], F32, name="by_y")
        weight_n = keep.tile([P, BLOCKS, D], F32, name="weight_n")
        turned = keep.tile([P, 2, BLOCKS, D], F32, name="turned")
        coef = keep.tile([P, 2, BLOCKS, D], F32, name="coef")
        whole = [P, 2, BLOCKS, D]
        nc.vector.tensor_scalar(side[:], rest[:, 0, :, 0], 0.0, 2 * NUDGE, IS_GE, MULT)
        nc.vector.tensor_tensor(by_y[:], rest[:], rest[:, 1:2, :, 0:1].to_broadcast(whole), MULT)
        nc.vector.scalar_tensor_tensor(pivot[:], side[:], -NUDGE, rest[:, 0, :, 0], ADD, ADD)
        nc.vector.tensor_tensor(by_x[:], rest[:], pivot[:].unsqueeze(1).unsqueeze(3).to_broadcast(whole), MULT)
        nc.vector.tensor_tensor(turned[:, 0], by_x[:, 0], by_y[:, 1], ADD)
        nc.vector.tensor_tensor(turned[:, 1], by_x[:, 1], by_y[:, 0], SUB)
        for b in range(BLOCKS):
            nc.scalar.activation(inv_len[:, b : b + 1], pivot[:, b : b + 1], ACT.Abs_reciprocal_sqrt, scale=pivot[:, b : b + 1], bias=by_y[:, 1, b, 0:1])
        for b in range(BLOCKS):
            nc.scalar.activation(weight_n[:, b, :], weight[:, b, :], ACT.Copy, scale=inv_len[:, b : b + 1])
        interleave(0)

        picked_bytes = keep.tile([P, S], U8, name="picked_bytes", align_bytes=64)
        dealt_bytes = keep.tile([P, BLOCKS, D, P], U8, name="dealt_bytes", align_bytes=64)
        nc.vector.tensor_copy(picked_bytes[:], byte_table[:].indirect(offsets[:]))
        nc.vector.tensor_tensor(
            coef[:].rearrange("p c b d -> p c (b d)"),
            turned[:].rearrange("p c b d -> p c (b d)"),
            weight_n[:].rearrange("p b d -> p (b d)").unsqueeze(1).to_broadcast([P, 2, BLOCKS * D]),
            MULT,
        )
        picked_words = [keep.tile([P, D, P], U32, name=f"picked_words{b}", align_bytes=64) for b in range(BLOCKS)]
        cols_per_block = S // 16 // BLOCKS

        def gather_words(b):
            part = offsets[:, b * cols_per_block : (b + 1) * cols_per_block]
            nc.vector.tensor_copy(picked_words[b][:].rearrange("p d i -> p i d"), word_table[:].bitcast(U32).indirect(part))

        def deal_bytes(b):
            nc.vector.tensor_copy(dealt_bytes[:, b], picked_bytes[:, b * D * P : (b + 1) * D * P].rearrange("p (i d) -> p d i", d=D))

        prods = keep.tile([P, 3, BLOCKS, D], F32, name="prods")
        sums = keep.tile([P, 3, BLOCKS], F32, name="sums")
        form = keep.tile([P, 3, BLOCKS], F32, name="form")
        diff = keep.tile([P, BLOCKS], F32, name="diff")
        minus_b = keep.tile([P, BLOCKS], F32, name="minus_b")
        c_eps = keep.tile([P, BLOCKS], F32, name="c_eps")
        deal_bytes(0)
        nc.vector.tensor_tensor(prods[:, 0:2], turned[:], coef[:], MULT)
        nc.vector.tensor_tensor(prods[:, 2], turned[:, 1], coef[:, 0], MULT)
        quantize(0)
        nc.vector.tensor_reduce(sums[:], prods[:], mybir.AxisListType.X, ADD)
        for b in range(BLOCKS):
            nc.scalar.activation(form[:, :, b], sums[:, :, b], ACT.Copy, scale=inv_len[:, b : b + 1])
        for b in range(BLOCKS):
            nc.scalar.activation(diff[:, b : b + 1], form[:, 1, b : b + 1], ACT.Identity, scale=-1.0, bias=form[:, 0, b : b + 1])
        nc.scalar.activation(minus_b[:], form[:, 2], ACT.Copy, scale=-1.0)
        nc.scalar.activation(c_eps[:], form[:, 1], ACT.Copy, scale=-EPS)
        interleave(1)
        gather_words(0)
        deal_bytes(1)
        gather_words(1)
        quantize(1)

        banks = [[psum.tile([P, 2, N], F32, name=f"yz{b}{e}", tag=f"bank{D * b + e}") for e in range(D)] for b in range(BLOCKS)]

        def yz(b, i, d):
            return banks[0][2 * i + d // 2][:, d % 2] if b == 0 else banks[1][d][:, i]

        def product(dst, b, d, cols):
            nc.tensor.matmul_mx(
                out=dst,
                lhsT=picked_words[b][:, d, :].bitcast(FP8X4),
                lhsT_scale=dealt_bytes[:, b, d, :],
                rhs=w_codes[:, cols].bitcast(FP8X4),
                rhs_scale=w_bytes[:, cols],
                start=True,
                stop=True,
            )

        sums_yz = [keep.tile([P, 2, 2, N], F32, name=f"sums_yz{b}") for b in range(BLOCKS)]
        rot = [keep.tile([P, 2, N], F32, name=f"rot{b}") for b in range(BLOCKS)]
        y_sq = [keep.tile([P, D, N], F32, name=f"y_sq{b}") for b in range(BLOCKS)]
        energy = [keep.tile([P, D, N], F32, name=f"energy{b}") for b in range(BLOCKS)]
        rot_sq = [keep.tile([P, 2, N], F32, name=f"rot_sq{b}") for b in range(BLOCKS)]
        norm_sq = [keep.tile([P, N], F32, name=f"norm_sq{b}") for b in range(BLOCKS)]
        inv = [keep.tile([P, N], F32, name=f"inv{b}") for b in range(BLOCKS)]
        inv_sq = [keep.tile([P, N], F32, name=f"inv_sq{b}") for b in range(BLOCKS)]
        level = [keep.tile([P, N], F32, name=f"level{b}") for b in range(BLOCKS)]
        quad = [keep.tile([P, N], F32, name=f"quad{b}") for b in range(BLOCKS)]
        unit = [keep.tile([P, 2, N], F32, name=f"unit{b}") for b in range(BLOCKS)]
        cross = [keep.tile([P, 2, N], F32, name=f"cross{b}") for b in range(BLOCKS)]
        result = [keep.tile([P, HALVES, P], F32, name=f"result{b}") for b in range(BLOCKS)]
        acc = [None] * BLOCKS

        def square_pair(e):
            nc.scalar.activation(y_sq[0][:, 2 * e : 2 * e + 2], banks[0][e][:], ACT.Square)

        def square_y(b, d):
            nc.scalar.activation(y_sq[b][:, d], yz(b, 0, d), ACT.Square)

        def weigh(b, d):
            bias = form[:, 1, b : b + 1] if d == D - 1 else 0.0
            if (b, d) in ((0, 0), (0, 1), (0, 2), (0, 3)):
                nc.gpsimd.tensor_scalar(energy[b][:, d], y_sq[b][:, d], weight[:, b, d : d + 1], bias, MULT, ADD)
            else:
                func = ACT.Identity if d == D - 1 else ACT.Copy
                nc.scalar.activation(energy[b][:, d], y_sq[b][:, d], func, scale=weight[:, b, d : d + 1], bias=bias)

        def add_terms(b, terms, first, last):
            for t, term in enumerate(terms):
                for h in range(HALVES):
                    nc.tensor.matmul(
                        acc[b][:, h, :],
                        lhsT=term[:, h * P : (h + 1) * P],
                        rhs=ident[:],
                        is_transpose=True,
                        start=first and t == 0 and h == 0,
                        stop=last and t == len(terms) - 1 and h == HALVES - 1,
                    )

        def head(b, c, i):
            nc.scalar.activation(sums_yz[b][:, c, i], yz(b, i, c), ACT.Copy, scale=coef[:, c, b, c : c + 1])

        def mac(dst, b, i, c, d, prev, op=ADD):
            nc.vector.scalar_tensor_tensor(dst, yz(b, i, d), coef[:, c, b, d : d + 1], prev, MULT, op)

        def sum_up(b, i):
            for c, d in ((1, 2), (0, 2), (1, 3), (0, 3), (0, 1)):
                mac(sums_yz[b][:, c, i], b, i, c, d, sums_yz[b][:, c, i])

        by_b = keep.tile([P, D - 1, 2, N], F32, name="by_b")
        part = keep.tile([P, 2, N], F32, name="part")

        def scale_bank(dst, c, d):
            nc.scalar.activation(dst, banks[1][d][:], ACT.Copy, scale=coef[:, c, 1, d : d + 1])

        def mac_bank(c, d, prev):
            nc.vector.scalar_tensor_tensor(sums_yz[1][:, c], banks[1][d][:], coef[:, c, 1, d : d + 1], prev, MULT, ADD)

        def combine(engine, b):
            engine.tensor_tensor(rot[b][:, 0], sums_yz[b][:, 0, 0], sums_yz[b][:, 1, 1], ADD)
            engine.tensor_tensor(rot[b][:, 1], sums_yz[b][:, 0, 1], sums_yz[b][:, 1, 0], SUB)

        def square_rot(b):
            nc.scalar.activation(rot_sq[b][:], rot[b][:], ACT.Square)

        def norm(engine, b):
            engine.tensor_tensor(norm_sq[b][:], rot_sq[b][:, 0], rot_sq[b][:, 1], ADD)

        def invert(b):
            nc.scalar.activation(inv[b][:], norm_sq[b][:], ACT.Abs_reciprocal_sqrt, bias=EPS)
            nc.scalar.activation(inv_sq[b][:], inv[b][:], ACT.Square)

        def make_level(b):
            nc.scalar.activation(level[b][:], rot_sq[b][:, 0], ACT.Identity, scale=diff[:, b : b + 1], bias=c_eps[:, b : b + 1])

        def normalise(b):
            nc.vector.tensor_tensor(unit[b][:], rot[b][:], inv[b][:].unsqueeze(1).to_broadcast([P, 2, N]), MULT)

        def fold(b):
            nc.vector.scalar_tensor_tensor(sums_yz[b][:, 0, 0], unit[b][:, 1], minus_b[:, b : b + 1], sums_yz[b][:, 0, 0], MULT, SUB)

        def quad_term(b):
            nc.vector.tensor_tensor(quad[b][:], level[b][:], inv_sq[b][:], MULT)

        def cross_terms(b, cs):
            nc.vector.scalar_tensor_tensor(cross[b][:, cs], sums_yz[b][:, cs, 0], 2.0, unit[b][:, cs], MULT, MULT)

        def finish(b, terms):
            add_terms(b, terms, False, True)
            nc.scalar.copy(result[b][:], acc[b][:])
            nc.sync.dma_start(out.rearrange("(h p) v -> p h v", p=P)[:, :, b * P : (b + 1) * P], result[b][:])

        def open_acc(b):
            acc[b] = psum.tile([P, HALVES, P], F32, name=f"acc{b}", tag=f"bank{b}")
            add_terms(b, [energy[b][:, d] for d in range(D)], True, False)

        for i in range(2):
            for d in range(D):
                product(yz(0, i, d), 0, d, slice(i * N, (i + 1) * N))
        for d in range(D):
            product(banks[1][d][:].rearrange("p i n -> p (i n)"), 1, d, slice(0, 2 * N))
        head(0, 0, 0)
        head(0, 1, 0)
        square_pair(0)
        head(0, 0, 1)
        head(0, 1, 1)
        sum_up(0, 0)
        square_pair(1)
        scale_bank(sums_yz[1][:, 0], 0, 0)
        scale_bank(sums_yz[1][:, 1], 1, 1)
        square_y(1, 1)
        square_y(1, 0)
        sum_up(0, 1)
        combine(nc.gpsimd, 0)
        square_rot(0)
        mac_bank(0, 2, sums_yz[1][:, 0])
        mac_bank(1, 2, sums_yz[1][:, 1])
        mac_bank(0, 3, sums_yz[1][:, 0])
        norm(nc.vector, 0)
        invert(0)
        make_level(0)
        mac_bank(1, 3, sums_yz[1][:, 1])
        mac_bank(0, 1, sums_yz[1][:, 0])
        combine(nc.vector, 1)
        square_rot(1)
        normalise(0)
        quad_term(0)
        fold(0)
        norm(nc.vector, 1)
        invert(1)
        make_level(1)
        cross_terms(0, slice(0, 2))
        normalise(1)
        quad_term(1)
        fold(1)
        cross_terms(1, slice(1, 2))
        cross_terms(1, slice(0, 1))
        square_y(1, 2)
        square_y(1, 3)
        weigh(0, 0)
        weigh(0, 1)
        weigh(0, 2)
        weigh(0, 3)
        weigh(1, 0)
        weigh(1, 1)
        weigh(1, 2)
        weigh(1, 3)
        open_acc(0)
        open_acc(1)
        finish(0, [quad[0], cross[0][:, 0], cross[0][:, 1]])
        finish(1, [quad[1], cross[1][:, 1], cross[1][:, 0]])
